import numpy as np
import ml_dtypes


def mxq(x, axis, fmt="e4m3"):
    dtype, down = {"e4m3": (ml_dtypes.float8_e4m3fn, 7), "e5m2": (ml_dtypes.float8_e5m2, 14)}[fmt]
    v = np.moveaxis(np.asarray(x, np.float32).astype(ml_dtypes.bfloat16).astype(np.float64), axis, -1)
    blocks = v.reshape(v.shape[:-1] + (-1, 32))
    amax = np.abs(blocks).max(-1, keepdims=True)
    byte = np.maximum(np.where(amax > 0, np.frexp(amax)[1] - 1 + 127, 0) - down, 1)
    scale = np.exp2(byte - 127.0)
    codes = (blocks / scale).astype(np.float32).astype(dtype).astype(np.float64)
    return np.moveaxis((codes * scale).reshape(v.shape), -1, axis)


WIDE = False


def mx_kscale(k):
    if not WIDE:
        return np.ones(k)
    levels = np.array([10, -10, 5, -5, 0])
    if k % 512:
        return np.exp2(np.random.permutation(np.resize(levels, k // 32))).repeat(32)
    a = np.empty((k // 512, 16))
    for p in range(k // 512):
        a[p, :8] = np.random.permutation(np.resize(levels, 8))
        for g in range(8):
            far = levels[np.abs(levels - a[p, g]) >= 10]
            a[p, g + 8] = far[np.random.randint(len(far))]
    return np.exp2(a.ravel()).repeat(32)


def f64(x):
    return np.asarray(x).astype(np.float64)


def striped(idx):
    return np.tile(idx.reshape(-1, 16).T, (8, 1)).astype(np.uint16)


def unstriped(offs):
    return offs[:16].T.reshape(-1).astype(np.int64)


E2M1 = np.array([0.0, 0.5, 1.0, 1.5, 2.0, 3.0, 4.0, 6.0, -0.0, -0.5, -1.0, -1.5, -2.0, -3.0, -4.0, -6.0])


def pack_weight(w, fmt):
    k, n = w.shape
    w = f64(np.asarray(w, np.float32).astype(ml_dtypes.bfloat16)).reshape(k // 32, 32, n)
    amax = np.abs(w).max(1)
    if fmt == "e4m3":
        byte = np.frexp(amax)[1] - 1 + 127 - 7
    else:
        mant, ex = np.frexp(amax / 6.0)
        byte = np.where(mant > 0.5, ex, ex - 1) + 127
    byte = np.clip(np.where(amax > 0, byte, 1), 1, 254)
    scaled = (w * np.exp2(127.0 - byte)[:, None, :]).reshape(k, n).astype(np.float32)
    by_word = np.ascontiguousarray(scaled.reshape(k // 512, 128, 4, n).transpose(0, 1, 3, 2))
    if fmt == "e4m3":
        words = by_word.astype(ml_dtypes.float8_e4m3fn).view(np.uint8)
    else:
        c = by_word.astype(ml_dtypes.float4_e2m1fn).view(np.uint8) & 0xF
        words = (c[..., 0::2] | (c[..., 1::2] << 4)).reshape(k // 512, 128, 2 * n)
    return np.ascontiguousarray(words), np.ascontiguousarray(byte.astype(np.uint8).reshape(k // 512, 16, n))


def unpack_weight(words, scales, fmt):
    g, _, n = scales.shape
    words = np.ascontiguousarray(words).reshape(g, 128, n, -1)
    if fmt == "e4m3":
        vals = words.view(ml_dtypes.float8_e4m3fn).astype(np.float64)
    else:
        nib = np.empty((g, 128, n, 4), np.uint8)
        nib[..., 0::2] = words & 0xF
        nib[..., 1::2] = words >> 4
        vals = E2M1[nib]
    vals = vals * np.repeat(np.exp2(scales.astype(np.float64) - 127.0), 8, axis=1)[..., None]
    return vals.transpose(0, 1, 3, 2).reshape(g * 512, n)


def pack_table4(v):
    words, scales = pack_weight(v, "e2m1")
    g, t = words.shape[0] // 2, v.shape[1]
    words = words.reshape(g, 2, 128, t, 2).transpose(0, 2, 3, 1, 4)
    return np.concatenate([words.reshape(g, -1), scales.reshape(g, -1)], axis=1)


def unpack_table4(tab):
    g, t = tab.shape[0], tab.shape[1] // 544
    words = tab[:, :512 * t].reshape(g, 128, t, 2, 2).transpose(0, 3, 1, 2, 4).reshape(2 * g, 128, 2 * t)
    return unpack_weight(words, tab[:, 512 * t:].reshape(2 * g, 16, t), "e2m1")


def silu(v):
    return v / (1.0 + np.exp(-np.maximum(v, -700.0)))


K, M, T, S = 1024, 128, 2048, 1024


def setup_inputs():
    n = np.random.standard_normal
    s = mx_kscale(K)[:, None]
    return {
        "tab": pack_table4(n((K, T)) * s),
        "w": (n((K, M)) / np.sqrt(K) / s).astype(np.float32),
        "b": (0.3 * n(128)).astype(np.float32),
        "offs": striped(np.random.permutation(T)[:S]),
    }


def reference(tab, w, b, offs):
    tab_ = unpack_table4(tab)[:, unstriped(offs)]
    w_ = mxq(f64(w), 0, "e4m3")
    y = tab_.T @ w_
    return silu(y + f64(b)[None, :])

@@ -1,0 +1,159 @@
+import concourse.mybir as mybir
+from concourse.masks import make_identity
+
+K, M, T, S = 1024, 128, 2048, 1024
+FLOPS = 2 * K * M * S
+
+F32 = mybir.dt.float32
+BF16 = mybir.dt.bfloat16
+I32 = mybir.dt.int32
+U32 = mybir.dt.uint32
+U16 = mybir.dt.uint16
+U8 = mybir.dt.uint8
+FP8X4 = mybir.dt.float8_e4m3fn_x4
+FP4X4 = mybir.dt.float4_e2m1fn_x4
+SILU = mybir.ActivationFunctionType.Silu
+COPY = mybir.ActivationFunctionType.Copy
+ADD = mybir.AluOpType.add
+
+P = 128
+WORD_BYTES = 512 * T
+BLOCKS = ((0, 256), (256, 256), (512, 256), (768, 256))
+
+
+def tile_list_tab4_tm_silu_kernel(tc, tab, w, b, offs, out):
+    nc = tc.nc
+    with (
+        tc.tile_pool(name="held", bufs=1) as held,
+        tc.psum_pool(name="psum", bufs=1) as psum,
+    ):
+        offsets = held.tile([P, S // 16], U16, name="offsets")
+        scale_tab = held.tile([P, T], U8, name="scale_tab", align_bytes=64)
+        word_tab = held.tile([P, T], I32, name="word_tab", align_bytes=64)
+        w_raw = held.tile([P, 2, 4, M], F32, name="w_raw", align_bytes=64)
+        w_grp = held.tile([P, 2, M, 4], BF16, name="w_grp", align_bytes=64)
+        w_codes = held.tile([P, 2, M], U32, name="w_codes", align_bytes=64)
+        w_scales = held.tile([P, 2, M], U8, name="w_scales", align_bytes=64)
+        b_col = held.tile([P, 1], F32, name="b_col")
+        b_row = held.tile([P, M], F32, name="b_row", align_bytes=64)
+        ident = held.tile([P, P], F32, name="ident", align_bytes=64)
+        warm = held.tile([P, 1], F32, name="warm")
+        picked = held.tile([P, S], U8, name="picked", align_bytes=64)
+        plane0 = held.tile([P, S], U8, name="plane0", align_bytes=64)
+        plane1 = held.tile([P, S], U8, name="plane1", align_bytes=64)
+        planes = (plane0, plane1)
+
+        nc.sync.dma_start(offsets[:], offs)
+        scale_rows = tab[0, WORD_BYTES : WORD_BYTES + 32 * T].rearrange("(q t) -> q t", t=T)
+        nc.sync.dma_start(scale_tab[0:32, :].bitcast(I32), scale_rows.bitcast(I32))
+        for h in range(2):
+            nc.sync.dma_start(w_raw[:, h].rearrange("p i n -> p (i n)"), w[512 * h : 512 * h + 512, :].rearrange("(p i) n -> p (i n)", i=4))
+        nc.gpsimd.dma_start(b_col[:], b.rearrange("(p o) -> p o", o=1))
+        nc.sync.dma_start(word_tab[:], tab[0, 0:WORD_BYTES].rearrange("(p x) -> p x", p=P).bitcast(I32))
+        nc.vector.memset(scale_tab[32:64, :].bitcast(I32), 0)
+        nc.vector.memset(scale_tab[64:128, :].bitcast(I32), 0)
+        nc.vector.memset(plane0[:].bitcast(I32), 0)
+        nc.vector.memset(plane1[:].bitcast(I32), 0)
+
+        nc.gpsimd.memset(warm[:], 0.0)
+        nc.scalar.activation(warm[:], warm[:], SILU)
+        make_identity(nc, ident[:])
+
+        nc.vector.tensor_copy(picked[:], scale_tab[:].indirect(offsets[:]))
+        for h in range(2):
+            for q in range(4):
+                nc.sync.dma_start(planes[h][32 * q : 32 * q + 4, :].bitcast(I32), picked[16 * h + 4 * q : 16 * h + 4 * q + 4, :].bitcast(I32))
+
+        for h in range(2):
+            nc.scalar.activation(w_grp[:, h], w_raw[:, h].rearrange("p i n -> p n i"), COPY)
+
+        words = []
+        codes = []
+        for t0, n in BLOCKS:
+            g = held.tile([P, n], U32, name=f"g{t0}", align_bytes=64)
+            words.append(g)
+            cd = held.tile([P, 2, n], U16, name=f"cd{t0}", align_bytes=64)
+            codes.append(cd)
+
+        def gather(s):
+            t0, n = BLOCKS[s]
+            nc.vector.tensor_copy(words[s][:], word_tab[:].bitcast(U32).indirect(offsets[:, t0 // 16 : (t0 + n) // 16]))
+
+        def part(s, a, n):
+            nc.vector.tensor_copy(codes[s][:, :, a : a + n], words[s][:, a : a + n].bitcast(U16).rearrange("p (t h) -> p h t", h=2))
+
+        def table_operand(s, h, a, n):
+            t0, total = BLOCKS[s]
+            raw = codes[s][:].rearrange("p h t -> p (h t)").bitcast(U8)
+            b0 = 2 * (h * total + a)
+            return raw[:, b0 : b0 + 2 * n].bitcast(FP4X4), planes[h][:, t0 + a : t0 + a + n]
+
+        def channels_multiply(s):
+            t0, n = BLOCKS[s]
+            acc = psum.tile([P, n], F32, name=f"acc{t0}")
+            for a in range(0, n, P):
+                for h in range(2):
+                    codes_ap, scales_ap = table_operand(s, h, a, P)
+                    nc.tensor.matmul_mx(out=acc[:, a : a + P], lhsT=w_codes[:, h, :].bitcast(FP8X4), lhsT_scale=w_scales[:, h, :],
+                                        rhs=codes_ap, rhs_scale=scales_ap, start=(h == 0), stop=(h == 1))
+            yt = held.tile([P, n], F32, name=f"yt{t0}", align_bytes=64)
+            nc.scalar.activation(yt[:], acc[:], SILU, bias=b_col[:])
+            return yt
+
+        def turn(s, yt, by_vector):
+            t0, n = BLOCKS[s]
+            turned = psum.tile([P, n // P, M], F32, name=f"turned{s % 2}")
+            for c in range(n // P):
+                nc.tensor.transpose(turned[:, c, :], yt[:, c * P : (c + 1) * P], ident[:])
+            o = held.tile([P, n // P, M], F32, name=f"o{t0}", align_bytes=64)
+            if by_vector:
+                nc.vector.tensor_copy(o[:], turned[:])
+            else:
+                nc.scalar.copy(o[:], turned[:])
+            nc.sync.dma_start(out[t0 : t0 + n, :].rearrange("(c p) n -> p c n", p=P), o[:])
+
+        def multiply(s, a, n):
+            t0, total = BLOCKS[s]
+            acc = psum.tile([P, n // P, M], F32, name=f"acc{t0 + a}")
+            for c in range(n // P):
+                for h in range(2):
+                    codes_ap, scales_ap = table_operand(s, h, a + c * P, P)
+                    nc.tensor.matmul_mx(out=acc[:, c, :], lhsT=codes_ap, lhsT_scale=scales_ap,
+                                        rhs=w_codes[:, h, :].bitcast(FP8X4), rhs_scale=w_scales[:, h, :], start=(h == 0), stop=(h == 1))
+            return acc
+
+        def finish(s, a, n, acc):
+            t0, total = BLOCKS[s]
+            y = held.tile([P, n // P, M], F32, name=f"y{t0 + a}", align_bytes=64)
+            o = held.tile([P, n // P, M], F32, name=f"o{t0 + a}", align_bytes=64)
+            nc.vector.tensor_tensor(y[:], acc[:], b_row[:].unsqueeze(1).to_broadcast([P, n // P, M]), ADD)
+            nc.scalar.activation(o[:], y[:], SILU)
+            nc.sync.dma_start(out[t0 + a : t0 + a + n, :].rearrange("(c p) n -> p c n", p=P), o[:])
+
+        nc.vector.quantize_mx(
+            out=w_codes[:].rearrange("p h n -> p (h n)").bitcast(FP8X4),
+            scales=w_scales[:].rearrange("p h n -> p (h n)"),
+            in_=w_grp[:].rearrange("p h n i -> p (h n i)"),
+        )
+        gather(0)
+        part(0, 0, 256)
+        yt0 = channels_multiply(0)
+        gather(1)
+        turn(0, yt0, False)
+        part(1, 0, 256)
+        yt1 = channels_multiply(1)
+        gather(2)
+        turn(1, yt1, False)
+        b_bank = psum.tile([P, M], F32, name="b_bank")
+        nc.tensor.transpose(b_bank[:], b_col[:].to_broadcast([P, M]), ident[:])
+        nc.scalar.copy(b_row[:], b_bank[:])
+        part(2, 0, 256)
+        yt2 = channels_multiply(2)
+        gather(3)
+        part(3, 0, P)
+        acc3a = multiply(3, 0, P)
+        part(3, P, P)
+        acc3b = multiply(3, P, P)
+        finish(3, 0, P, acc3a)
+        finish(3, P, P, acc3b)
+        turn(2, yt2, True)

@@ -46,26 +46,27 @@ def tile_list_tab4_tm_silu_kernel(tc, tab, w, b, offs, out):
         nc.sync.dma_start(offsets[:], offs)
         scale_rows = tab[0, WORD_BYTES : WORD_BYTES + 32 * T].rearrange("(q t) -> q t", t=T)
         nc.sync.dma_start(scale_tab[0:32, :].bitcast(I32), scale_rows.bitcast(I32))
-        for h in range(2):
-            nc.sync.dma_start(w_raw[:, h].rearrange("p i n -> p (i n)"), w[512 * h : 512 * h + 512, :].rearrange("(p i) n -> p (i n)", i=4))
-        nc.gpsimd.dma_start(b_col[:], b.rearrange("(p o) -> p o", o=1))
         nc.sync.dma_start(word_tab[:], tab[0, 0:WORD_BYTES].rearrange("(p x) -> p x", p=P).bitcast(I32))
+        nc.sync.dma_start(w_raw[:].rearrange("p h i n -> p h (i n)"), w.rearrange("(h p i) n -> p h (i n)", h=2, i=4))
+        nc.gpsimd.dma_start(b_col[:], b.rearrange("(p o) -> p o", o=1))
         nc.vector.memset(scale_tab[32:64, :].bitcast(I32), 0)
         nc.vector.memset(scale_tab[64:128, :].bitcast(I32), 0)
-        nc.vector.memset(plane0[:].bitcast(I32), 0)
-        nc.vector.memset(plane1[:].bitcast(I32), 0)
-
-        nc.gpsimd.memset(warm[:], 0.0)
+        nc.vector.memset(warm[:], 0.0)
         nc.scalar.activation(warm[:], warm[:], SILU)
-        make_identity(nc, ident[:])
 
         nc.vector.tensor_copy(picked[:], scale_tab[:].indirect(offsets[:]))
         for h in range(2):
             for q in range(4):
-                nc.sync.dma_start(planes[h][32 * q : 32 * q + 4, :].bitcast(I32), picked[16 * h + 4 * q : 16 * h + 4 * q + 4, :].bitcast(I32))
+                queue = nc.sync if h == 0 else nc.gpsimd if q == 0 else nc.scalar
+                queue.dma_start(planes[h][32 * q : 32 * q + 4, :].bitcast(I32), picked[16 * h + 4 * q : 16 * h + 4 * q + 4, :].bitcast(I32))
 
         for h in range(2):
             nc.scalar.activation(w_grp[:, h], w_raw[:, h].rearrange("p i n -> p n i"), COPY)
+
+        make_identity(nc, ident[:])
+        b_bank = psum.tile([P, M], F32, name="b_bank", tag="acc0")
+        nc.tensor.transpose(b_bank[:], b_col[:].to_broadcast([P, M]), ident[:])
+        nc.scalar.copy(b_row[:], b_bank[:])
 
         words = []
         codes = []
@@ -88,33 +89,9 @@ def tile_list_tab4_tm_silu_kernel(tc, tab, w, b, offs, out):
             b0 = 2 * (h * total + a)
             return raw[:, b0 : b0 + 2 * n].bitcast(FP4X4), planes[h][:, t0 + a : t0 + a + n]
 
-        def channels_multiply(s):
-            t0, n = BLOCKS[s]
-            acc = psum.tile([P, n], F32, name=f"acc{t0}")
-            for a in range(0, n, P):
-                for h in range(2):
-                    codes_ap, scales_ap = table_operand(s, h, a, P)
-                    nc.tensor.matmul_mx(out=acc[:, a : a + P], lhsT=w_codes[:, h, :].bitcast(FP8X4), lhsT_scale=w_scales[:, h, :],
-                                        rhs=codes_ap, rhs_scale=scales_ap, start=(h == 0), stop=(h == 1))
-            yt = held.tile([P, n], F32, name=f"yt{t0}", align_bytes=64)
-            nc.scalar.activation(yt[:], acc[:], SILU, bias=b_col[:])
-            return yt
-
-        def turn(s, yt, by_vector):
-            t0, n = BLOCKS[s]
-            turned = psum.tile([P, n // P, M], F32, name=f"turned{s % 2}")
-            for c in range(n // P):
-                nc.tensor.transpose(turned[:, c, :], yt[:, c * P : (c + 1) * P], ident[:])
-            o = held.tile([P, n // P, M], F32, name=f"o{t0}", align_bytes=64)
-            if by_vector:
-                nc.vector.tensor_copy(o[:], turned[:])
-            else:
-                nc.scalar.copy(o[:], turned[:])
-            nc.sync.dma_start(out[t0 : t0 + n, :].rearrange("(c p) n -> p c n", p=P), o[:])
-
         def multiply(s, a, n):
             t0, total = BLOCKS[s]
-            acc = psum.tile([P, n // P, M], F32, name=f"acc{t0 + a}")
+            acc = psum.tile([P, n // P, M], F32, name=f"acc{t0 + a}", tag=f"acc{t0 + a}")
             for c in range(n // P):
                 for h in range(2):
                     codes_ap, scales_ap = table_operand(s, h, a + c * P, P)
@@ -130,30 +107,27 @@ def tile_list_tab4_tm_silu_kernel(tc, tab, w, b, offs, out):
             nc.scalar.activation(o[:], y[:], SILU)
             nc.sync.dma_start(out[t0 + a : t0 + a + n, :].rearrange("(c p) n -> p c n", p=P), o[:])
 
+        gather(0)
+        part(0, 0, 256)
+        gather(1)
+        part(1, 0, 256)
         nc.vector.quantize_mx(
             out=w_codes[:].rearrange("p h n -> p (h n)").bitcast(FP8X4),
             scales=w_scales[:].rearrange("p h n -> p (h n)"),
             in_=w_grp[:].rearrange("p h n i -> p (h n i)"),
         )
-        gather(0)
-        part(0, 0, 256)
-        yt0 = channels_multiply(0)
-        gather(1)
-        turn(0, yt0, False)
-        part(1, 0, 256)
-        yt1 = channels_multiply(1)
+        acc0 = multiply(0, 0, 256)
+        acc1 = multiply(1, 0, 256)
         gather(2)
-        turn(1, yt1, False)
-        b_bank = psum.tile([P, M], F32, name="b_bank")
-        nc.tensor.transpose(b_bank[:], b_col[:].to_broadcast([P, M]), ident[:])
-        nc.scalar.copy(b_row[:], b_bank[:])
         part(2, 0, 256)
-        yt2 = channels_multiply(2)
+        acc2 = multiply(2, 0, 256)
         gather(3)
+        finish(0, 0, 256, acc0)
         part(3, 0, P)
         acc3a = multiply(3, 0, P)
         part(3, P, P)
         acc3b = multiply(3, P, P)
+        finish(1, 0, 256, acc1)
+        finish(2, 0, 256, acc2)
         finish(3, 0, P, acc3a)
         finish(3, P, P, acc3b)
-        turn(2, yt2, True)

import concourse.mybir as mybir
from concourse.masks import make_identity

K, M, T, S = 1024, 128, 2048, 1024
FLOPS = 2 * K * M * S

F32 = mybir.dt.float32
BF16 = mybir.dt.bfloat16
I32 = mybir.dt.int32
U32 = mybir.dt.uint32
U16 = mybir.dt.uint16
U8 = mybir.dt.uint8
FP8X4 = mybir.dt.float8_e4m3fn_x4
FP4X4 = mybir.dt.float4_e2m1fn_x4
SILU = mybir.ActivationFunctionType.Silu
COPY = mybir.ActivationFunctionType.Copy
ADD = mybir.AluOpType.add

P = 128
WORD_BYTES = 512 * T
BLOCKS = ((0, 256), (256, 256), (512, 256), (768, 256))


def tile_list_tab4_tm_silu_kernel(tc, tab, w, b, offs, out):
    nc = tc.nc
    with (
        tc.tile_pool(name="held", bufs=1) as held,
        tc.psum_pool(name="psum", bufs=1) as psum,
    ):
        offsets = held.tile([P, S // 16], U16, name="offsets")
        scale_tab = held.tile([P, T], U8, name="scale_tab", align_bytes=64)
        word_tab = held.tile([P, T], I32, name="word_tab", align_bytes=64)
        w_raw = held.tile([P, 2, 4, M], F32, name="w_raw", align_bytes=64)
        w_grp = held.tile([P, 2, M, 4], BF16, name="w_grp", align_bytes=64)
        w_codes = held.tile([P, 2, M], U32, name="w_codes", align_bytes=64)
        w_scales = held.tile([P, 2, M], U8, name="w_scales", align_bytes=64)
        b_col = held.tile([P, 1], F32, name="b_col")
        b_row = held.tile([P, M], F32, name="b_row", align_bytes=64)
        ident = held.tile([P, P], F32, name="ident", align_bytes=64)
        warm = held.tile([P, 1], F32, name="warm")
        picked = held.tile([P, S], U8, name="picked", align_bytes=64)
        plane0 = held.tile([P, S], U8, name="plane0", align_bytes=64)
        plane1 = held.tile([P, S], U8, name="plane1", align_bytes=64)
        planes = (plane0, plane1)

        nc.sync.dma_start(offsets[:], offs)
        scale_rows = tab[0, WORD_BYTES : WORD_BYTES + 32 * T].rearrange("(q t) -> q t", t=T)
        nc.sync.dma_start(scale_tab[0:32, :].bitcast(I32), scale_rows.bitcast(I32))
        nc.sync.dma_start(word_tab[:], tab[0, 0:WORD_BYTES].rearrange("(p x) -> p x", p=P).bitcast(I32))
        nc.sync.dma_start(w_raw[:].rearrange("p h i n -> p h (i n)"), w.rearrange("(h p i) n -> p h (i n)", h=2, i=4))
        nc.gpsimd.dma_start(b_col[:], b.rearrange("(p o) -> p o", o=1))
        nc.vector.memset(scale_tab[32:64, :].bitcast(I32), 0)
        nc.vector.memset(scale_tab[64:128, :].bitcast(I32), 0)
        nc.vector.memset(warm[:], 0.0)
        nc.scalar.activation(warm[:], warm[:], SILU)

        nc.vector.tensor_copy(picked[:], scale_tab[:].indirect(offsets[:]))
        for h in range(2):
            for q in range(4):
                queue = nc.sync if h == 0 else nc.gpsimd if q == 0 else nc.scalar
                queue.dma_start(planes[h][32 * q : 32 * q + 4, :].bitcast(I32), picked[16 * h + 4 * q : 16 * h + 4 * q + 4, :].bitcast(I32))

        for h in range(2):
            nc.scalar.activation(w_grp[:, h], w_raw[:, h].rearrange("p i n -> p n i"), COPY)

        make_identity(nc, ident[:])
        b_bank = psum.tile([P, M], F32, name="b_bank", tag="acc0")
        nc.tensor.transpose(b_bank[:], b_col[:].to_broadcast([P, M]), ident[:])
        nc.scalar.copy(b_row[:], b_bank[:])

        words = []
        codes = []
        for t0, n in BLOCKS:
            g = held.tile([P, n], U32, name=f"g{t0}", align_bytes=64)
            words.append(g)
            cd = held.tile([P, 2, n], U16, name=f"cd{t0}", align_bytes=64)
            codes.append(cd)

        def gather(s):
            t0, n = BLOCKS[s]
            nc.vector.tensor_copy(words[s][:], word_tab[:].bitcast(U32).indirect(offsets[:, t0 // 16 : (t0 + n) // 16]))

        def part(s, a, n):
            nc.vector.tensor_copy(codes[s][:, :, a : a + n], words[s][:, a : a + n].bitcast(U16).rearrange("p (t h) -> p h t", h=2))

        def table_operand(s, h, a, n):
            t0, total = BLOCKS[s]
            raw = codes[s][:].rearrange("p h t -> p (h t)").bitcast(U8)
            b0 = 2 * (h * total + a)
            return raw[:, b0 : b0 + 2 * n].bitcast(FP4X4), planes[h][:, t0 + a : t0 + a + n]

        def multiply(s, a, n):
            t0, total = BLOCKS[s]
            acc = psum.tile([P, n // P, M], F32, name=f"acc{t0 + a}", tag=f"acc{t0 + a}")
            for c in range(n // P):
                for h in range(2):
                    codes_ap, scales_ap = table_operand(s, h, a + c * P, P)
                    nc.tensor.matmul_mx(out=acc[:, c, :], lhsT=codes_ap, lhsT_scale=scales_ap,
                                        rhs=w_codes[:, h, :].bitcast(FP8X4), rhs_scale=w_scales[:, h, :], start=(h == 0), stop=(h == 1))
            return acc

        def finish(s, a, n, acc):
            t0, total = BLOCKS[s]
            y = held.tile([P, n // P, M], F32, name=f"y{t0 + a}", align_bytes=64)
            o = held.tile([P, n // P, M], F32, name=f"o{t0 + a}", align_bytes=64)
            nc.vector.tensor_tensor(y[:], acc[:], b_row[:].unsqueeze(1).to_broadcast([P, n // P, M]), ADD)
            nc.scalar.activation(o[:], y[:], SILU)
            nc.sync.dma_start(out[t0 + a : t0 + a + n, :].rearrange("(c p) n -> p c n", p=P), o[:])

        gather(0)
        part(0, 0, 256)
        gather(1)
        part(1, 0, 256)
        nc.vector.quantize_mx(
            out=w_codes[:].rearrange("p h n -> p (h n)").bitcast(FP8X4),
            scales=w_scales[:].rearrange("p h n -> p (h n)"),
            in_=w_grp[:].rearrange("p h n i -> p (h n i)"),
        )
        acc0 = multiply(0, 0, 256)
        acc1 = multiply(1, 0, 256)
        gather(2)
        part(2, 0, 256)
        acc2 = multiply(2, 0, 256)
        gather(3)
        finish(0, 0, 256, acc0)
        part(3, 0, P)
        acc3a = multiply(3, 0, P)
        part(3, P, P)
        acc3b = multiply(3, P, P)
        finish(1, 0, 256, acc1)
        finish(2, 0, 256, acc2)
        finish(3, 0, P, acc3a)
        finish(3, P, P, acc3b)
